import numpy as np
import ml_dtypes


def mxq(x, axis, fmt="e4m3"):
    dtype, down = {"e4m3": (ml_dtypes.float8_e4m3fn, 7), "e5m2": (ml_dtypes.float8_e5m2, 14)}[fmt]
    v = np.moveaxis(np.asarray(x, np.float32).astype(ml_dtypes.bfloat16).astype(np.float64), axis, -1)
    blocks = v.reshape(v.shape[:-1] + (-1, 32))
    amax = np.abs(blocks).max(-1, keepdims=True)
    byte = np.maximum(np.where(amax > 0, np.frexp(amax)[1] - 1 + 127, 0) - down, 1)
    scale = np.exp2(byte - 127.0)
    codes = (blocks / scale).astype(np.float32).astype(dtype).astype(np.float64)
    return np.moveaxis((codes * scale).reshape(v.shape), -1, axis)


WIDE = False


def mx_kscale(k):
    if not WIDE:
        return np.ones(k)
    levels = np.array([10, -10, 5, -5, 0])
    if k % 512:
        return np.exp2(np.random.permutation(np.resize(levels, k // 32))).repeat(32)
    a = np.empty((k // 512, 16))
    for p in range(k // 512):
        a[p, :8] = np.random.permutation(np.resize(levels, 8))
        for g in range(8):
            far = levels[np.abs(levels - a[p, g]) >= 10]
            a[p, g + 8] = far[np.random.randint(len(far))]
    return np.exp2(a.ravel()).repeat(32)


def f64(x):
    return np.asarray(x).astype(np.float64)


def striped(idx):
    return np.tile(np.asarray(idx).reshape(-1, 16).T, (8, 1)).astype(np.uint16)


def unstriped(offs):
    return offs[:16].T.reshape(-1).astype(np.int64)


E2M1 = np.array([0.0, 0.5, 1.0, 1.5, 2.0, 3.0, 4.0, 6.0, -0.0, -0.5, -1.0, -1.5, -2.0, -3.0, -4.0, -6.0])


def pack_weight(w, fmt):
    k, n = w.shape
    w = f64(np.asarray(w, np.float32).astype(ml_dtypes.bfloat16)).reshape(k // 32, 32, n)
    amax = np.abs(w).max(1)
    if fmt == "e4m3":
        byte = np.frexp(amax)[1] - 1 + 127 - 7
    else:
        mant, ex = np.frexp(amax / 6.0)
        byte = np.where(mant > 0.5, ex, ex - 1) + 127
    byte = np.clip(np.where(amax > 0, byte, 1), 1, 254)
    scaled = (w * np.exp2(127.0 - byte)[:, None, :]).reshape(k, n).astype(np.float32)
    by_word = np.ascontiguousarray(scaled.reshape(k // 512, 128, 4, n).transpose(0, 1, 3, 2))
    if fmt == "e4m3":
        words = by_word.astype(ml_dtypes.float8_e4m3fn).view(np.uint8)
    else:
        c = by_word.astype(ml_dtypes.float4_e2m1fn).view(np.uint8) & 0xF
        words = (c[..., 0::2] | (c[..., 1::2] << 4)).reshape(k // 512, 128, 2 * n)
    return np.ascontiguousarray(words), np.ascontiguousarray(byte.astype(np.uint8).reshape(k // 512, 16, n))


def unpack_weight(words, scales, fmt):
    g, _, n = scales.shape
    words = np.ascontiguousarray(words).reshape(g, 128, n, -1)
    if fmt == "e4m3":
        vals = words.view(ml_dtypes.float8_e4m3fn).astype(np.float64)
    else:
        nib = np.empty((g, 128, n, 4), np.uint8)
        nib[..., 0::2] = words & 0xF
        nib[..., 1::2] = words >> 4
        vals = E2M1[nib]
    vals = vals * np.repeat(np.exp2(scales.astype(np.float64) - 127.0), 8, axis=1)[..., None]
    return vals.transpose(0, 1, 3, 2).reshape(g * 512, n)


B, N, T, D, NQ = 1, 1024, 4096, 1024, 128
SEG = 32


def setup_inputs():
    n = np.random.standard_normal
    pages = np.random.permutation(T // 32)[:B * N // 32]
    idx = (pages[:, None] * 32 + np.arange(32)[None, :]).reshape(-1)
    s = mx_kscale(D)[:, None]
    kp = pack_weight(n((D, T)) / s, "e2m1")
    return {
        "qT": (n((B, D, NQ)) * s * (1.00 / np.sqrt(D))).astype(np.float32),
        "k_words": np.ascontiguousarray(kp[0].reshape(1, 2, 128, T, 2).transpose(0, 2, 3, 1, 4)).reshape(1, 128, T, 4),
        "k_scales": kp[1],
        "offs": striped(idx),
    }


def reference(qT, k_words, k_scales, offs):
    idx = unstriped(offs)
    pick = lambda x, which: x[:, which].reshape(x.shape[0], B, -1).transpose(1, 0, 2)
    k = unpack_weight(k_words.reshape(1, 128, T, 2, 2).transpose(0, 3, 1, 2, 4).reshape(2, 128, 2 * T), k_scales, "e2m1")
    kg = pick(k, idx)
    qq = mxq(f64(qT), 1, "e4m3")
    a = qq.transpose(0, 2, 1) @ kg
    y = np.log(np.exp(2.0 * a).reshape(B, NQ, N // SEG, SEG).sum(-1))
    return y

@@ -1,0 +1,151 @@
+from contextlib import ExitStack
+
+import concourse.mybir as mybir
+
+F32 = mybir.dt.float32
+BF16 = mybir.dt.bfloat16
+I32 = mybir.dt.int32
+U32 = mybir.dt.uint32
+U16 = mybir.dt.uint16
+U8 = mybir.dt.uint8
+FP8X4 = mybir.dt.float8_e4m3fn_x4
+FP4X4 = mybir.dt.float4_e2m1fn_x4
+ALU = mybir.AluOpType
+ACT = mybir.ActivationFunctionType
+AXIS_X = mybir.AxisListType.X
+
+P = 128
+PACK = 4
+PASSES = 2
+T = 4096
+N = 1024
+NQ = 128
+PAGE = 32
+PAGES = N // PAGE
+HALF = 512
+CHUNK = 128
+CHUNK_PAGES = CHUNK // PAGE
+CHUNKS = N // CHUNK
+AHEAD = 4
+WIDE_CHUNKS = 2
+
+FLOPS = 2 * NQ * N * PASSES * P * PACK
+
+
+def tile_attend_pagelse_kernel(tc, qT, k_words, k_scales, offs, out):
+    nc = tc.nc
+    with ExitStack() as ctx:
+        held = ctx.enter_context(tc.tile_pool(name="held", bufs=1))
+        ring = ctx.enter_context(tc.tile_pool(name="ring", bufs=AHEAD))
+        psum = ctx.enter_context(tc.psum_pool(name="psum", bufs=1))
+
+        offsets = held.tile([P, N // 16], U16, name="offsets")
+        q_raw = held.tile([P, PASSES, PACK, NQ], F32, name="q_raw")
+        q_bf = held.tile([P, PASSES, NQ, PACK], BF16, name="q_bf", align_bytes=64)
+        q_codes = held.tile([P, PASSES * NQ], U32, name="q_codes", align_bytes=64)
+        q_scales = held.tile([P, PASSES * NQ], U8, name="q_scales", align_bytes=64)
+        pool_words = held.tile([P, T], I32, name="pool_words", align_bytes=64)
+        pool_scales = held.tile([P, T], U8, name="pool_scales", align_bytes=64)
+        picked_scales = held.tile([P, N], U8, name="picked_scales", align_bytes=64)
+        k_planes = held.tile([P, PASSES, N], U8, name="k_planes", align_bytes=64)
+
+        nc.sync.dma_start(offsets[:], offs)
+        nc.sync.dma_start(pool_scales[0:32, :].bitcast(I32), k_scales.rearrange("o f t -> (o f) t").bitcast(I32))
+        nc.sync.dma_start(
+            q_raw[:].rearrange("p g j q -> p g (j q)"),
+            qT[0].rearrange("(g p j) q -> p g (j q)", g=PASSES, j=PACK),
+        )
+        nc.sync.dma_start(pool_words[:], k_words[0].rearrange("p t b -> p (t b)").bitcast(I32))
+        nc.vector.memset(pool_scales[32:64, :].bitcast(I32), 0)
+        nc.vector.memset(pool_scales[64:P, :].bitcast(I32), 0)
+        nc.vector.memset(k_planes[:].rearrange("p o n -> p (o n)").bitcast(I32), 0)
+
+        nc.vector.tensor_copy(picked_scales[:], pool_scales[:].indirect(offsets[:]))
+        for o in range(PASSES):
+            for quad in range(4):
+                row = 16 * o + 4 * quad
+                if row > 0:
+                    nc.scalar.dma_start(
+                        k_planes[32 * quad : 32 * quad + 4, o, :].bitcast(I32),
+                        picked_scales[row : row + 4, :].bitcast(I32),
+                    )
+        nc.vector.tensor_copy(k_planes[0:4, 0, :].bitcast(I32), picked_scales[0:4, :].bitcast(I32))
+        nc.vector.tensor_scalar(
+            q_bf[:], q_raw[:].rearrange("p g j q -> p g q j"), 2.0, None, ALU.mult
+        )
+        nc.vector.quantize_mx(
+            out=q_codes[:].bitcast(FP8X4), scales=q_scales[:], in_=q_bf[:].rearrange("p g q j -> p (g q j)")
+        )
+
+        neg_max = held.tile([P, PAGES], F32, name="neg_max")
+        sums = held.tile([P, PAGES], F32, name="sums")
+        weights = held.tile([P, N], F32, name="weights")
+        shifted = held.tile([P, N], F32, name="shifted")
+
+        picked = []
+        for half in range(N // HALF):
+            picked.append(held.tile([P, HALF], U32, name="picked%d" % half, align_bytes=64))
+            lists = offsets[:, half * HALF // 16 : (half + 1) * HALF // 16]
+            nc.vector.tensor_copy(picked[half][:], pool_words[:].bitcast(U32).indirect(lists))
+
+        def score(chunk):
+            slot0 = chunk * CHUNK
+            words = picked[slot0 // HALF][:, slot0 % HALF : slot0 % HALF + CHUNK]
+            keys = ring.tile([P, PASSES, CHUNK], U16, name="keys", align_bytes=64)
+            nc.vector.tensor_copy(keys[:], words.bitcast(U16).rearrange("p (n o) -> p o n", o=PASSES))
+            bank = psum.tile([P, CHUNK], F32, name="bank%d" % chunk)
+            for o in range(PASSES):
+                nc.tensor.matmul_mx(
+                    out=bank[:],
+                    lhsT=q_codes[:, o * NQ : (o + 1) * NQ].bitcast(FP8X4),
+                    lhsT_scale=q_scales[:, o * NQ : (o + 1) * NQ],
+                    rhs=keys[:, o, :].bitcast(FP4X4),
+                    rhs_scale=k_planes[:, o, slot0 : slot0 + CHUNK],
+                    start=(o == 0),
+                    stop=(o == PASSES - 1),
+                )
+            return bank
+
+        def weigh(chunk, bank):
+            pages = slice(chunk * CHUNK_PAGES, (chunk + 1) * CHUNK_PAGES)
+            slots = slice(chunk * CHUNK, (chunk + 1) * CHUNK)
+            by_page = bank[:].rearrange("p (j i) -> p j i", i=PAGE)
+            nc.vector.tensor_reduce(neg_max[:, pages], by_page, AXIS_X, ALU.max, negate=True)
+            if chunk < CHUNKS - WIDE_CHUNKS:
+                for j in range(CHUNK_PAGES):
+                    page = pages.start + j
+                    nc.scalar.activation(
+                        weights[:, page * PAGE : (page + 1) * PAGE],
+                        bank[:, j * PAGE : (j + 1) * PAGE],
+                        ACT.Exp,
+                        bias=neg_max[:, page : page + 1],
+                        accum_out=sums[:, page : page + 1],
+                    )
+            else:
+                nc.vector.tensor_tensor(
+                    shifted[:, slots].rearrange("p (j i) -> p j i", i=PAGE),
+                    by_page,
+                    neg_max[:, pages].unsqueeze(2).to_broadcast([P, CHUNK_PAGES, PAGE]),
+                    ALU.add,
+                )
+                nc.scalar.activation(weights[:, slots], shifted[:, slots], ACT.Exp)
+
+        banks = []
+        for step in range(CHUNKS + AHEAD):
+            if step >= AHEAD:
+                weigh(step - AHEAD, banks[step - AHEAD])
+            if step < CHUNKS:
+                banks.append(score(step))
+        wide0 = CHUNKS - WIDE_CHUNKS
+        nc.vector.tensor_reduce(
+            sums[:, wide0 * CHUNK_PAGES :],
+            weights[:, wide0 * CHUNK :].rearrange("p (j i) -> p j i", i=PAGE),
+            AXIS_X,
+            ALU.add,
+        )
+
+        result = held.tile([P, PAGES], F32, name="result")
+        logs = held.tile([P, PAGES], F32, name="logs")
+        nc.scalar.activation(logs[:], sums[:], ACT.Ln)
+        nc.vector.tensor_tensor(result[:], logs[:], neg_max[:], ALU.subtract)
+        nc.sync.dma_start(out[0], result[:])

@@ -27,7 +27,8 @@ CHUNK = 128
 CHUNK_PAGES = CHUNK // PAGE
 CHUNKS = N // CHUNK
 AHEAD = 4
-WIDE_CHUNKS = 2
+LAST_PAGES = 8
+ROW0 = (0, 16)
 
 FLOPS = 2 * NQ * N * PASSES * P * PACK
 
@@ -49,44 +50,52 @@ def tile_attend_pagelse_kernel(tc, qT, k_words, k_scales, offs, out):
         picked_scales = held.tile([P, N], U8, name="picked_scales", align_bytes=64)
         k_planes = held.tile([P, PASSES, N], U8, name="k_planes", align_bytes=64)
 
-        nc.sync.dma_start(offsets[:], offs)
-        nc.sync.dma_start(pool_scales[0:32, :].bitcast(I32), k_scales.rearrange("o f t -> (o f) t").bitcast(I32))
-        nc.sync.dma_start(
-            q_raw[:].rearrange("p g j q -> p g (j q)"),
-            qT[0].rearrange("(g p j) q -> p g (j q)", g=PASSES, j=PACK),
-        )
-        nc.sync.dma_start(pool_words[:], k_words[0].rearrange("p t b -> p (t b)").bitcast(I32))
+        def load_q(o):
+            rows = qT[0, o * P * PACK : (o + 1) * P * PACK, :]
+            nc.sync.dma_start(q_raw[:, o], rows.rearrange("(p j) q -> p j q", j=PACK))
+
+        def quantize_q(o):
+            cols = slice(o * NQ, (o + 1) * NQ)
+            nc.scalar.activation(q_bf[:, o], q_raw[:, o].rearrange("p j q -> p q j"), ACT.Copy, scale=2.0)
+            nc.vector.quantize_mx(
+                out=q_codes[:, cols].bitcast(FP8X4),
+                scales=q_scales[:, cols],
+                in_=q_bf[:, o].rearrange("p q j -> p (q j)"),
+            )
+
         nc.vector.memset(pool_scales[32:64, :].bitcast(I32), 0)
         nc.vector.memset(pool_scales[64:P, :].bitcast(I32), 0)
         nc.vector.memset(k_planes[:].rearrange("p o n -> p (o n)").bitcast(I32), 0)
+        nc.sync.dma_start(offsets[:], offs)
+        nc.sync.dma_start(pool_scales[0:32, :].bitcast(I32), k_scales.rearrange("o f t -> (o f) t").bitcast(I32))
+        load_q(0)
+        nc.sync.dma_start(pool_words[:], k_words[0].rearrange("p t b -> p (t b)").bitcast(I32))
+        load_q(1)
 
         nc.vector.tensor_copy(picked_scales[:], pool_scales[:].indirect(offsets[:]))
+        quantize_q(0)
         for o in range(PASSES):
             for quad in range(4):
-                row = 16 * o + 4 * quad
-                if row > 0:
-                    nc.scalar.dma_start(
-                        k_planes[32 * quad : 32 * quad + 4, o, :].bitcast(I32),
-                        picked_scales[row : row + 4, :].bitcast(I32),
-                    )
-        nc.vector.tensor_copy(k_planes[0:4, 0, :].bitcast(I32), picked_scales[0:4, :].bitcast(I32))
-        nc.vector.tensor_scalar(
-            q_bf[:], q_raw[:].rearrange("p g j q -> p g q j"), 2.0, None, ALU.mult
-        )
-        nc.vector.quantize_mx(
-            out=q_codes[:].bitcast(FP8X4), scales=q_scales[:], in_=q_bf[:].rearrange("p g q j -> p (g q j)")
-        )
+                row = ROW0[o] + 4 * quad
+                source = picked_scales[row : row + 4, :].bitcast(I32)
+                target = k_planes[32 * quad : 32 * quad + 4, o, :].bitcast(I32)
+                if row == 0:
+                    nc.vector.tensor_copy(target, source)
+                elif row == 4:
+                    nc.gpsimd.dma_start(target, source)
+                else:
+                    nc.scalar.dma_start(target, source)
 
         neg_max = held.tile([P, PAGES], F32, name="neg_max")
         sums = held.tile([P, PAGES], F32, name="sums")
         weights = held.tile([P, N], F32, name="weights")
-        shifted = held.tile([P, N], F32, name="shifted")
 
         picked = []
         for half in range(N // HALF):
             picked.append(held.tile([P, HALF], U32, name="picked%d" % half, align_bytes=64))
             lists = offsets[:, half * HALF // 16 : (half + 1) * HALF // 16]
             nc.vector.tensor_copy(picked[half][:], pool_words[:].bitcast(U32).indirect(lists))
+        quantize_q(1)
 
         def score(chunk):
             slot0 = chunk * CHUNK
@@ -108,27 +117,16 @@ def tile_attend_pagelse_kernel(tc, qT, k_words, k_scales, offs, out):
 
         def weigh(chunk, bank):
             pages = slice(chunk * CHUNK_PAGES, (chunk + 1) * CHUNK_PAGES)
-            slots = slice(chunk * CHUNK, (chunk + 1) * CHUNK)
             by_page = bank[:].rearrange("p (j i) -> p j i", i=PAGE)
             nc.vector.tensor_reduce(neg_max[:, pages], by_page, AXIS_X, ALU.max, negate=True)
-            if chunk < CHUNKS - WIDE_CHUNKS:
-                for j in range(CHUNK_PAGES):
-                    page = pages.start + j
-                    nc.scalar.activation(
-                        weights[:, page * PAGE : (page + 1) * PAGE],
-                        bank[:, j * PAGE : (j + 1) * PAGE],
-                        ACT.Exp,
-                        bias=neg_max[:, page : page + 1],
-                        accum_out=sums[:, page : page + 1],
-                    )
-            else:
-                nc.vector.tensor_tensor(
-                    shifted[:, slots].rearrange("p (j i) -> p j i", i=PAGE),
-                    by_page,
-                    neg_max[:, pages].unsqueeze(2).to_broadcast([P, CHUNK_PAGES, PAGE]),
-                    ALU.add,
+            for j in range(CHUNK_PAGES):
+                page = pages.start + j
+                nc.scalar.activation(
+                    weights[:, page * PAGE : (page + 1) * PAGE],
+                    by_page[:, j, :],
+                    ACT.Exp,
+                    bias=neg_max[:, page : page + 1],
                 )
-                nc.scalar.activation(weights[:, slots], shifted[:, slots], ACT.Exp)
 
         banks = []
         for step in range(CHUNKS + AHEAD):
@@ -136,13 +134,11 @@ def tile_attend_pagelse_kernel(tc, qT, k_words, k_scales, offs, out):
                 weigh(step - AHEAD, banks[step - AHEAD])
             if step < CHUNKS:
                 banks.append(score(step))
-        wide0 = CHUNKS - WIDE_CHUNKS
-        nc.vector.tensor_reduce(
-            sums[:, wide0 * CHUNK_PAGES :],
-            weights[:, wide0 * CHUNK :].rearrange("p (j i) -> p j i", i=PAGE),
-            AXIS_X,
-            ALU.add,
-        )
+        for pages in (slice(0, PAGES - LAST_PAGES), slice(PAGES - LAST_PAGES, PAGES)):
+            slots = slice(pages.start * PAGE, pages.stop * PAGE)
+            nc.vector.tensor_reduce(
+                sums[:, pages], weights[:, slots].rearrange("p (j i) -> p j i", i=PAGE), AXIS_X, ALU.add
+            )
 
         result = held.tile([P, PAGES], F32, name="result")
         logs = held.tile([P, PAGES], F32, name="logs")

@@ -26,7 +26,8 @@ HALF = 512
 CHUNK = 128
 CHUNK_PAGES = CHUNK // PAGE
 CHUNKS = N // CHUNK
-AHEAD = 4
+AHEAD = 5
+EARLY = 2
 LAST_PAGES = 8
 ROW0 = (0, 16)
 
@@ -56,7 +57,12 @@ def tile_attend_pagelse_kernel(tc, qT, k_words, k_scales, offs, out):
 
         def quantize_q(o):
             cols = slice(o * NQ, (o + 1) * NQ)
-            nc.scalar.activation(q_bf[:, o], q_raw[:, o].rearrange("p j q -> p q j"), ACT.Copy, scale=2.0)
+            nc.scalar.activation(
+                q_bf[:, o].rearrange("p (c i) j -> p c j i", i=PACK),
+                q_raw[:, o].rearrange("p j (c i) -> p c j i", i=PACK),
+                ACT.Copy,
+                scale=2.0,
+            )
             nc.vector.quantize_mx(
                 out=q_codes[:, cols].bitcast(FP8X4),
                 scales=q_scales[:, cols],
@@ -81,7 +87,7 @@ def tile_attend_pagelse_kernel(tc, qT, k_words, k_scales, offs, out):
                 target = k_planes[32 * quad : 32 * quad + 4, o, :].bitcast(I32)
                 if row == 0:
                     nc.vector.tensor_copy(target, source)
-                elif row == 4:
+                elif row == 28:
                     nc.gpsimd.dma_start(target, source)
                 else:
                     nc.scalar.dma_start(target, source)
@@ -95,13 +101,16 @@ def tile_attend_pagelse_kernel(tc, qT, k_words, k_scales, offs, out):
             picked.append(held.tile([P, HALF], U32, name="picked%d" % half, align_bytes=64))
             lists = offsets[:, half * HALF // 16 : (half + 1) * HALF // 16]
             nc.vector.tensor_copy(picked[half][:], pool_words[:].bitcast(U32).indirect(lists))
-        quantize_q(1)
 
-        def score(chunk):
+        def split(chunk):
             slot0 = chunk * CHUNK
             words = picked[slot0 // HALF][:, slot0 % HALF : slot0 % HALF + CHUNK]
             keys = ring.tile([P, PASSES, CHUNK], U16, name="keys", align_bytes=64)
             nc.vector.tensor_copy(keys[:], words.bitcast(U16).rearrange("p (n o) -> p o n", o=PASSES))
+            return keys
+
+        def score(chunk, keys):
+            slot0 = chunk * CHUNK
             bank = psum.tile([P, CHUNK], F32, name="bank%d" % chunk)
             for o in range(PASSES):
                 nc.tensor.matmul_mx(
@@ -128,12 +137,14 @@ def tile_attend_pagelse_kernel(tc, qT, k_words, k_scales, offs, out):
                     bias=neg_max[:, page : page + 1],
                 )
 
-        banks = []
-        for step in range(CHUNKS + AHEAD):
+        early = [split(chunk) for chunk in range(EARLY)]
+        quantize_q(1)
+        banks = [score(chunk, early[chunk]) for chunk in range(EARLY)]
+        for step in range(EARLY, CHUNKS + AHEAD):
             if step >= AHEAD:
                 weigh(step - AHEAD, banks[step - AHEAD])
             if step < CHUNKS:
-                banks.append(score(step))
+                banks.append(score(step, split(step)))
         for pages in (slice(0, PAGES - LAST_PAGES), slice(PAGES - LAST_PAGES, PAGES)):
             slots = slice(pages.start * PAGE, pages.stop * PAGE)
             nc.vector.tensor_reduce(

from contextlib import ExitStack

import concourse.mybir as mybir

F32 = mybir.dt.float32
BF16 = mybir.dt.bfloat16
I32 = mybir.dt.int32
U32 = mybir.dt.uint32
U16 = mybir.dt.uint16
U8 = mybir.dt.uint8
FP8X4 = mybir.dt.float8_e4m3fn_x4
FP4X4 = mybir.dt.float4_e2m1fn_x4
ALU = mybir.AluOpType
ACT = mybir.ActivationFunctionType
AXIS_X = mybir.AxisListType.X

P = 128
PACK = 4
PASSES = 2
T = 4096
N = 1024
NQ = 128
PAGE = 32
PAGES = N // PAGE
HALF = 512
CHUNK = 128
CHUNK_PAGES = CHUNK // PAGE
CHUNKS = N // CHUNK
AHEAD = 5
EARLY = 2
LAST_PAGES = 8
ROW0 = (0, 16)

FLOPS = 2 * NQ * N * PASSES * P * PACK


def tile_attend_pagelse_kernel(tc, qT, k_words, k_scales, offs, out):
    nc = tc.nc
    with ExitStack() as ctx:
        held = ctx.enter_context(tc.tile_pool(name="held", bufs=1))
        ring = ctx.enter_context(tc.tile_pool(name="ring", bufs=AHEAD))
        psum = ctx.enter_context(tc.psum_pool(name="psum", bufs=1))

        offsets = held.tile([P, N // 16], U16, name="offsets")
        q_raw = held.tile([P, PASSES, PACK, NQ], F32, name="q_raw")
        q_bf = held.tile([P, PASSES, NQ, PACK], BF16, name="q_bf", align_bytes=64)
        q_codes = held.tile([P, PASSES * NQ], U32, name="q_codes", align_bytes=64)
        q_scales = held.tile([P, PASSES * NQ], U8, name="q_scales", align_bytes=64)
        pool_words = held.tile([P, T], I32, name="pool_words", align_bytes=64)
        pool_scales = held.tile([P, T], U8, name="pool_scales", align_bytes=64)
        picked_scales = held.tile([P, N], U8, name="picked_scales", align_bytes=64)
        k_planes = held.tile([P, PASSES, N], U8, name="k_planes", align_bytes=64)

        def load_q(o):
            rows = qT[0, o * P * PACK : (o + 1) * P * PACK, :]
            nc.sync.dma_start(q_raw[:, o], rows.rearrange("(p j) q -> p j q", j=PACK))

        def quantize_q(o):
            cols = slice(o * NQ, (o + 1) * NQ)
            nc.scalar.activation(
                q_bf[:, o].rearrange("p (c i) j -> p c j i", i=PACK),
                q_raw[:, o].rearrange("p j (c i) -> p c j i", i=PACK),
                ACT.Copy,
                scale=2.0,
            )
            nc.vector.quantize_mx(
                out=q_codes[:, cols].bitcast(FP8X4),
                scales=q_scales[:, cols],
                in_=q_bf[:, o].rearrange("p q j -> p (q j)"),
            )

        nc.vector.memset(pool_scales[32:64, :].bitcast(I32), 0)
        nc.vector.memset(pool_scales[64:P, :].bitcast(I32), 0)
        nc.vector.memset(k_planes[:].rearrange("p o n -> p (o n)").bitcast(I32), 0)
        nc.sync.dma_start(offsets[:], offs)
        nc.sync.dma_start(pool_scales[0:32, :].bitcast(I32), k_scales.rearrange("o f t -> (o f) t").bitcast(I32))
        load_q(0)
        nc.sync.dma_start(pool_words[:], k_words[0].rearrange("p t b -> p (t b)").bitcast(I32))
        load_q(1)

        nc.vector.tensor_copy(picked_scales[:], pool_scales[:].indirect(offsets[:]))
        quantize_q(0)
        for o in range(PASSES):
            for quad in range(4):
                row = ROW0[o] + 4 * quad
                source = picked_scales[row : row + 4, :].bitcast(I32)
                target = k_planes[32 * quad : 32 * quad + 4, o, :].bitcast(I32)
                if row == 0:
                    nc.vector.tensor_copy(target, source)
                elif row == 28:
                    nc.gpsimd.dma_start(target, source)
                else:
                    nc.scalar.dma_start(target, source)

        neg_max = held.tile([P, PAGES], F32, name="neg_max")
        sums = held.tile([P, PAGES], F32, name="sums")
        weights = held.tile([P, N], F32, name="weights")

        picked = []
        for half in range(N // HALF):
            picked.append(held.tile([P, HALF], U32, name="picked%d" % half, align_bytes=64))
            lists = offsets[:, half * HALF // 16 : (half + 1) * HALF // 16]
            nc.vector.tensor_copy(picked[half][:], pool_words[:].bitcast(U32).indirect(lists))

        def split(chunk):
            slot0 = chunk * CHUNK
            words = picked[slot0 // HALF][:, slot0 % HALF : slot0 % HALF + CHUNK]
            keys = ring.tile([P, PASSES, CHUNK], U16, name="keys", align_bytes=64)
            nc.vector.tensor_copy(keys[:], words.bitcast(U16).rearrange("p (n o) -> p o n", o=PASSES))
            return keys

        def score(chunk, keys):
            slot0 = chunk * CHUNK
            bank = psum.tile([P, CHUNK], F32, name="bank%d" % chunk)
            for o in range(PASSES):
                nc.tensor.matmul_mx(
                    out=bank[:],
                    lhsT=q_codes[:, o * NQ : (o + 1) * NQ].bitcast(FP8X4),
                    lhsT_scale=q_scales[:, o * NQ : (o + 1) * NQ],
                    rhs=keys[:, o, :].bitcast(FP4X4),
                    rhs_scale=k_planes[:, o, slot0 : slot0 + CHUNK],
                    start=(o == 0),
                    stop=(o == PASSES - 1),
                )
            return bank

        def weigh(chunk, bank):
            pages = slice(chunk * CHUNK_PAGES, (chunk + 1) * CHUNK_PAGES)
            by_page = bank[:].rearrange("p (j i) -> p j i", i=PAGE)
            nc.vector.tensor_reduce(neg_max[:, pages], by_page, AXIS_X, ALU.max, negate=True)
            for j in range(CHUNK_PAGES):
                page = pages.start + j
                nc.scalar.activation(
                    weights[:, page * PAGE : (page + 1) * PAGE],
                    by_page[:, j, :],
                    ACT.Exp,
                    bias=neg_max[:, page : page + 1],
                )

        early = [split(chunk) for chunk in range(EARLY)]
        quantize_q(1)
        banks = [score(chunk, early[chunk]) for chunk in range(EARLY)]
        for step in range(EARLY, CHUNKS + AHEAD):
            if step >= AHEAD:
                weigh(step - AHEAD, banks[step - AHEAD])
            if step < CHUNKS:
                banks.append(score(step, split(step)))
        for pages in (slice(0, PAGES - LAST_PAGES), slice(PAGES - LAST_PAGES, PAGES)):
            slots = slice(pages.start * PAGE, pages.stop * PAGE)
            nc.vector.tensor_reduce(
                sums[:, pages], weights[:, slots].rearrange("p (j i) -> p j i", i=PAGE), AXIS_X, ALU.add
            )

        result = held.tile([P, PAGES], F32, name="result")
        logs = held.tile([P, PAGES], F32, name="logs")
        nc.scalar.activation(logs[:], sums[:], ACT.Ln)
        nc.vector.tensor_tensor(result[:], logs[:], neg_max[:], ALU.subtract)
        nc.sync.dma_start(out[0], result[:])
